import numpy as np
import ml_dtypes


def mxq(x, axis, fmt="e4m3"):
    dtype, down = {"e4m3": (ml_dtypes.float8_e4m3fn, 7), "e5m2": (ml_dtypes.float8_e5m2, 14)}[fmt]
    v = np.moveaxis(np.asarray(x, np.float32).astype(ml_dtypes.bfloat16).astype(np.float64), axis, -1)
    blocks = v.reshape(v.shape[:-1] + (-1, 32))
    amax = np.abs(blocks).max(-1, keepdims=True)
    byte = np.maximum(np.where(amax > 0, np.frexp(amax)[1] - 1 + 127, 0) - down, 1)
    scale = np.exp2(byte - 127.0)
    codes = (blocks / scale).astype(np.float32).astype(dtype).astype(np.float64)
    return np.moveaxis((codes * scale).reshape(v.shape), -1, axis)


WIDE = False


def mx_kscale(k):
    if not WIDE:
        return np.ones(k)
    levels = np.array([10, -10, 5, -5, 0])
    if k % 512:
        return np.exp2(np.random.permutation(np.resize(levels, k // 32))).repeat(32)
    a = np.empty((k // 512, 16))
    for p in range(k // 512):
        a[p, :8] = np.random.permutation(np.resize(levels, 8))
        for g in range(8):
            far = levels[np.abs(levels - a[p, g]) >= 10]
            a[p, g + 8] = far[np.random.randint(len(far))]
    return np.exp2(a.ravel()).repeat(32)


def f64(x):
    return np.asarray(x).astype(np.float64)


def striped(idx):
    return np.tile(idx.reshape(-1, 16).T, (8, 1)).astype(np.uint16)


def unstriped(offs):
    return offs[:16].T.reshape(-1).astype(np.int64)


def pack_weight(w):
    k, n = w.shape
    w = f64(np.asarray(w, np.float32).astype(ml_dtypes.bfloat16)).reshape(k // 32, 32, n)
    amax = np.abs(w).max(1)
    byte = np.clip(np.where(amax > 0, np.frexp(amax)[1] - 1 + 127 - 7, 1), 1, 254)
    scaled = (w * np.exp2(127.0 - byte)[:, None, :]).reshape(k, n).astype(np.float32)
    words = np.ascontiguousarray(scaled.reshape(k // 512, 128, 4, n).transpose(0, 1, 3, 2)).astype(ml_dtypes.float8_e4m3fn).view(np.uint8)
    return words, np.ascontiguousarray(byte.astype(np.uint8).reshape(k // 512, 16, n))


def unpack_weight(words, scales):
    g, p, n, _ = words.shape
    vals = np.ascontiguousarray(words).view(ml_dtypes.float8_e4m3fn).astype(np.float64) * np.repeat(np.exp2(scales.astype(np.float64) - 127.0), 8, axis=1)[..., None]
    return vals.transpose(0, 1, 3, 2).reshape(g * 512, n)


K, T, E, C, N = 1024, 512, 4, 256, 128


def by_expert(wq, xq):
    return np.concatenate([wq[e].T @ xq[:, e * C:(e + 1) * C] for e in range(E)], axis=1)


def setup_inputs():
    n = np.random.standard_normal
    s = mx_kscale(K)[:, None]
    first = np.random.permutation(np.repeat(np.arange(E), T // E))
    second = (first + 1 + np.random.permutation(np.repeat(np.arange(E - 1), -(-T // (E - 1)))[:T])) % E
    while np.bincount(second, minlength=E).max() != T // E:
        load = np.bincount(second, minlength=E); hi, lo = int(load.argmax()), int(load.argmin())
        t = np.flatnonzero((second == hi) & (first != lo))[0]; second[t] = lo
    slot_token = np.empty(E * C, np.int64); pos = np.empty((2, T), np.int64); fill = np.zeros(E, np.int64)
    place = np.stack([np.random.permutation(C) for _ in range(E)])
    for r, deal in enumerate((first, second)):
        for t in np.random.permutation(T):
            e = deal[t]; j = e * C + place[e, fill[e]]; fill[e] += 1; slot_token[j] = t; pos[r, t] = j
    g = np.random.uniform(0.2, 0.8, T)
    packed = [pack_weight(m) for m in n((E, K, N)) / np.sqrt(K) / s[None]]
    return {
        "xT": (n((K, T)) * s).astype(np.float32),
        "w_words": np.stack([m[0] for m in packed]),
        "w_scales": np.stack([m[1] for m in packed]),
        "gate": np.stack([np.tile(g, (N, 1)), np.tile(1.0 - g, (N, 1))]).astype(np.float32),
        "offs": striped(slot_token),
        "pos1": striped(pos[0]),
        "pos2": striped(pos[1]),
    }


def reference(xT, w_words, w_scales, gate, offs, pos1, pos2):
    idx = unstriped(offs)
    xq = mxq(f64(xT)[:, idx], 0, "e4m3")
    w = np.stack([unpack_weight(w_words[e], w_scales[e]) for e in range(E)])
    y = by_expert(w, xq)
    return f64(gate[0]) * y[:, unstriped(pos1)] + f64(gate[1]) * y[:, unstriped(pos2)]

@@ -1,0 +1,138 @@
+from contextlib import ExitStack
+
+import concourse.mybir as mybir
+
+K, T, E, C, N = 1024, 512, 4, 256, 128
+FLOPS = 2 * K * N * E * C
+
+P = 128
+PACK = 4
+PASSES = K // (P * PACK)
+SLOTS = E * C
+
+F32 = mybir.dt.float32
+BF16 = mybir.dt.bfloat16
+I32 = mybir.dt.int32
+U32 = mybir.dt.uint32
+U16 = mybir.dt.uint16
+U8 = mybir.dt.uint8
+FP8X4 = mybir.dt.float8_e4m3fn_x4
+MULT = mybir.AluOpType.mult
+ADD = mybir.AluOpType.add
+
+HALF = T // 2
+VSHARE = 168
+
+GROUPS = ((0, 256), (256, 256), (512, 256), (768, 128), (896, 128))
+CUTS = (384, 384, 256)
+LAST_CUTS = (384, 384, 192, 64)
+
+
+def tile_routed_moe_kernel(tc, xT, w_words, w_scales, gate, offs, pos1, pos2, out):
+    nc = tc.nc
+    with ExitStack() as ctx:
+        held = ctx.enter_context(tc.tile_pool(name="held", bufs=1))
+        psum = ctx.enter_context(tc.psum_pool(name="psum", bufs=1))
+
+        offs_sb = held.tile([P, SLOTS // 16], U16, name="offs_sb")
+        pos1_sb = held.tile([P, T // 16], U16, name="pos1_sb")
+        pos2_sb = held.tile([P, T // 16], U16, name="pos2_sb")
+        w_sb = held.tile([P, E, PASSES, N], U32, name="w_sb", align_bytes=64)
+        ws_sb = held.tile([P, E, PASSES, N], U8, name="ws_sb", align_bytes=64)
+        gate_sb = held.tile([P, 2, T], F32, name="gate_sb", align_bytes=64)
+        xs = held.tile([P, T], U8, name="xs", align_bytes=64)
+        gs = held.tile([P, SLOTS], U8, name="gs", align_bytes=64)
+        y_sb = held.tile([P, SLOTS], F32, name="y_sb", align_bytes=64)
+        raw = [[held.tile([P, PACK, HALF], F32, name=f"raw{a}{h}", align_bytes=64) for h in range(2)] for a in range(PASSES)]
+        grouped = [[held.tile([P, HALF, PACK], BF16, name=f"grouped{a}{h}", align_bytes=64) for h in range(2)] for a in range(PASSES)]
+        xw = [held.tile([P, T], U32, name=f"xw{a}", align_bytes=64) for a in range(PASSES)]
+        gw = [held.tile([P, SLOTS], U32, name=f"gw{a}", align_bytes=64) for a in range(PASSES)]
+
+        warm = held.tile([P, 8], F32, name="warm")
+        nc.vector.memset(warm[:], 0.0)
+        nc.scalar.copy(warm[:, 4:8], warm[:, 0:4])
+        nc.gpsimd.memset(xs[:], 0)
+        nc.vector.memset(ws_sb[:].rearrange("p e a n -> p (e a n)").bitcast(I32), 0)
+
+        def load_x(a, h):
+            rows = xT[512 * a : 512 * (a + 1), HALF * h : HALF * (h + 1)]
+            nc.sync.dma_start(out=raw[a][h][:], in_=rows.rearrange("(p t) n -> p t n", t=PACK))
+
+        load_x(0, 0)
+        load_x(0, 1)
+        nc.sync.dma_start(offs_sb[:], offs)
+        load_x(1, 0)
+        load_x(1, 1)
+        nc.sync.dma_start(
+            out=w_sb[:].rearrange("p e a n -> p (e a) n").bitcast(I32),
+            in_=w_words.rearrange("e a p n r -> p (e a) (n r)").bitcast(I32),
+        )
+        for q in range(4):
+            nc.sync.dma_start(
+                out=ws_sb[32 * q : 32 * q + 4].rearrange("p e a n -> p (e a) n").bitcast(I32),
+                in_=w_scales[:, :, 4 * q : 4 * q + 4, :].rearrange("e a r n -> r (e a) n").bitcast(I32),
+            )
+        nc.sync.dma_start(pos1_sb[:], pos1)
+        nc.sync.dma_start(pos2_sb[:], pos2)
+        nc.sync.dma_start(out=gate_sb[:], in_=gate.rearrange("s p n -> p s n"))
+
+        def interleave(copy, a, h, lo, hi):
+            copy(grouped[a][h][:, lo:hi, :], raw[a][h][:, :, lo:hi].rearrange("p t n -> p n t"))
+
+        def quantize(a, h):
+            cols = slice(HALF * h, HALF * (h + 1))
+            nc.vector.quantize_mx(
+                out=xw[a][:, cols].bitcast(FP8X4),
+                scales=xs[4 * a :, cols],
+                in_=grouped[a][h][:].rearrange("p n t -> p (n t)"),
+            )
+
+        def gather(dst, src, cuts):
+            lo = 0
+            for n in cuts:
+                nc.vector.tensor_copy(dst[:, lo : lo + n], src[:].indirect(offs_sb[:, lo // 16 : (lo + n) // 16]))
+                lo += n
+
+        for h in range(2):
+            interleave(nc.vector.tensor_copy, 0, h, 0, VSHARE)
+            interleave(nc.scalar.copy, 0, h, VSHARE, HALF)
+        for h in range(2):
+            quantize(0, h)
+        for h in range(2):
+            for lo in range(0, HALF, 128):
+                interleave(nc.scalar.copy, 1, h, lo, lo + 128)
+        gather(gw[0], xw[0], CUTS)
+        for h in range(2):
+            quantize(1, h)
+        gather(gs, xs, CUTS)
+        gather(gw[1], xw[1], LAST_CUTS)
+
+        banks = [psum.tile([P, n], F32, name=f"bank{i}") for i, (lo, n) in enumerate(GROUPS)]
+
+        for a in range(PASSES):
+            for i, (lo, n) in enumerate(GROUPS):
+                nc.tensor.matmul_mx(
+                    out=banks[i][:],
+                    lhsT=w_sb[:, lo // C, a, :].bitcast(FP8X4),
+                    lhsT_scale=ws_sb[:, lo // C, a, :],
+                    rhs=gw[a][:, lo : lo + n].bitcast(FP8X4),
+                    rhs_scale=gs[4 * a :, lo : lo + n],
+                    start=(a == 0),
+                    stop=(a == PASSES - 1),
+                )
+        for i, (lo, n) in enumerate(GROUPS):
+            nc.scalar.copy(y_sb[:, lo : lo + n], banks[i][:])
+
+        parts = [held.tile([P, 2, HALF], F32, name=f"part{h}", align_bytes=64) for h in range(2)]
+        results = [held.tile([P, HALF], F32, name=f"result{h}", align_bytes=64) for h in range(2)]
+        for h in range(2):
+            for s, pos in enumerate((pos1_sb, pos2_sb)):
+                nc.vector.tensor_tensor(
+                    parts[h][:, s, :],
+                    y_sb[:].indirect(pos[:, 16 * h : 16 * (h + 1)]),
+                    gate_sb[:, s, HALF * h : HALF * (h + 1)],
+                    MULT,
+                )
+        for h in range(2):
+            nc.vector.tensor_tensor(results[h][:], parts[h][:, 0, :], parts[h][:, 1, :], ADD)
+            nc.sync.dma_start(out=out[:, HALF * h : HALF * (h + 1)], in_=results[h][:])

@@ -21,7 +21,8 @@ MULT = mybir.AluOpType.mult
 ADD = mybir.AluOpType.add
 
 HALF = T // 2
-VSHARE = 168
+VEC_TOKENS = 304
+OUT_CUT = 320
 
 GROUPS = ((0, 256), (256, 256), (512, 256), (768, 128), (896, 128))
 CUTS = (384, 384, 256)
@@ -43,8 +44,9 @@ def tile_routed_moe_kernel(tc, xT, w_words, w_scales, gate, offs, pos1, pos2, ou
         xs = held.tile([P, T], U8, name="xs", align_bytes=64)
         gs = held.tile([P, SLOTS], U8, name="gs", align_bytes=64)
         y_sb = held.tile([P, SLOTS], F32, name="y_sb", align_bytes=64)
-        raw = [[held.tile([P, PACK, HALF], F32, name=f"raw{a}{h}", align_bytes=64) for h in range(2)] for a in range(PASSES)]
-        grouped = [[held.tile([P, HALF, PACK], BF16, name=f"grouped{a}{h}", align_bytes=64) for h in range(2)] for a in range(PASSES)]
+        raw0 = held.tile([P, PACK, T], F32, name="raw0", align_bytes=64)
+        raw1 = [held.tile([P, PACK, HALF], F32, name=f"raw1{h}", align_bytes=64) for h in range(2)]
+        grouped = [held.tile([P, T, PACK], BF16, name=f"grouped{a}", align_bytes=64) for a in range(PASSES)]
         xw = [held.tile([P, T], U32, name=f"xw{a}", align_bytes=64) for a in range(PASSES)]
         gw = [held.tile([P, SLOTS], U32, name=f"gw{a}", align_bytes=64) for a in range(PASSES)]
 
@@ -54,15 +56,11 @@ def tile_routed_moe_kernel(tc, xT, w_words, w_scales, gate, offs, pos1, pos2, ou
         nc.gpsimd.memset(xs[:], 0)
         nc.vector.memset(ws_sb[:].rearrange("p e a n -> p (e a n)").bitcast(I32), 0)
 
-        def load_x(a, h):
-            rows = xT[512 * a : 512 * (a + 1), HALF * h : HALF * (h + 1)]
-            nc.sync.dma_start(out=raw[a][h][:], in_=rows.rearrange("(p t) n -> p t n", t=PACK))
-
-        load_x(0, 0)
-        load_x(0, 1)
+        nc.sync.dma_start(out=raw0[:], in_=xT[0:512, :].rearrange("(p t) n -> p t n", t=PACK))
         nc.sync.dma_start(offs_sb[:], offs)
-        load_x(1, 0)
-        load_x(1, 1)
+        for h in range(2):
+            rows = xT[512:1024, HALF * h : HALF * (h + 1)]
+            nc.sync.dma_start(out=raw1[h][:], in_=rows.rearrange("(p t) n -> p t n", t=PACK))
         nc.sync.dma_start(
             out=w_sb[:].rearrange("p e a n -> p (e a) n").bitcast(I32),
             in_=w_words.rearrange("e a p n r -> p (e a) (n r)").bitcast(I32),
@@ -76,15 +74,15 @@ def tile_routed_moe_kernel(tc, xT, w_words, w_scales, gate, offs, pos1, pos2, ou
         nc.sync.dma_start(pos2_sb[:], pos2)
         nc.sync.dma_start(out=gate_sb[:], in_=gate.rearrange("s p n -> p s n"))
 
-        def interleave(copy, a, h, lo, hi):
-            copy(grouped[a][h][:, lo:hi, :], raw[a][h][:, :, lo:hi].rearrange("p t n -> p n t"))
+        def interleave(copy, dst, src):
+            copy(dst.rearrange("p (c i) t -> p c t i", i=4), src.rearrange("p t (c i) -> p c t i", i=4))
 
         def quantize(a, h):
             cols = slice(HALF * h, HALF * (h + 1))
             nc.vector.quantize_mx(
                 out=xw[a][:, cols].bitcast(FP8X4),
                 scales=xs[4 * a :, cols],
-                in_=grouped[a][h][:].rearrange("p n t -> p (n t)"),
+                in_=grouped[a][:, cols, :].rearrange("p n t -> p (n t)"),
             )
 
         def gather(dst, src, cuts):
@@ -93,14 +91,12 @@ def tile_routed_moe_kernel(tc, xT, w_words, w_scales, gate, offs, pos1, pos2, ou
                 nc.vector.tensor_copy(dst[:, lo : lo + n], src[:].indirect(offs_sb[:, lo // 16 : (lo + n) // 16]))
                 lo += n
 
-        for h in range(2):
-            interleave(nc.vector.tensor_copy, 0, h, 0, VSHARE)
-            interleave(nc.scalar.copy, 0, h, VSHARE, HALF)
+        for lo, hi, copy in ((0, HALF, nc.vector.tensor_copy), (HALF, VEC_TOKENS, nc.vector.tensor_copy), (VEC_TOKENS, T, nc.scalar.copy)):
+            interleave(copy, grouped[0][:, lo:hi, :], raw0[:, :, lo:hi])
         for h in range(2):
             quantize(0, h)
         for h in range(2):
-            for lo in range(0, HALF, 128):
-                interleave(nc.scalar.copy, 1, h, lo, lo + 128)
+            interleave(nc.scalar.copy, grouped[1][:, HALF * h : HALF * (h + 1), :], raw1[h][:])
         gather(gw[0], xw[0], CUTS)
         for h in range(2):
             quantize(1, h)
@@ -123,16 +119,15 @@ def tile_routed_moe_kernel(tc, xT, w_words, w_scales, gate, offs, pos1, pos2, ou
         for i, (lo, n) in enumerate(GROUPS):
             nc.scalar.copy(y_sb[:, lo : lo + n], banks[i][:])
 
-        parts = [held.tile([P, 2, HALF], F32, name=f"part{h}", align_bytes=64) for h in range(2)]
-        results = [held.tile([P, HALF], F32, name=f"result{h}", align_bytes=64) for h in range(2)]
-        for h in range(2):
-            for s, pos in enumerate((pos1_sb, pos2_sb)):
-                nc.vector.tensor_tensor(
-                    parts[h][:, s, :],
-                    y_sb[:].indirect(pos[:, 16 * h : 16 * (h + 1)]),
-                    gate_sb[:, s, HALF * h : HALF * (h + 1)],
-                    MULT,
-                )
-        for h in range(2):
-            nc.vector.tensor_tensor(results[h][:], parts[h][:, 0, :], parts[h][:, 1, :], ADD)
-            nc.sync.dma_start(out=out[:, HALF * h : HALF * (h + 1)], in_=results[h][:])
+        part1 = held.tile([P, T], F32, name="part1", align_bytes=64)
+        part2 = held.tile([P, T], F32, name="part2", align_bytes=64)
+        result = held.tile([P, T], F32, name="result", align_bytes=64)
+        spans = ((0, OUT_CUT), (OUT_CUT, T))
+        nc.vector.tensor_tensor(part1[:], y_sb[:].indirect(pos1_sb[:]), gate_sb[:, 0, :], MULT)
+        for lo, hi in spans:
+            nc.vector.tensor_tensor(
+                part2[:, lo:hi], y_sb[:].indirect(pos2_sb[:, lo // 16 : hi // 16]), gate_sb[:, 1, lo:hi], MULT
+            )
+        for lo, hi in spans:
+            nc.vector.tensor_tensor(result[:, lo:hi], part1[:, lo:hi], part2[:, lo:hi], ADD)
+            nc.sync.dma_start(out=out[:, lo:hi], in_=result[:, lo:hi])

from contextlib import ExitStack

import concourse.mybir as mybir

K, T, E, C, N = 1024, 512, 4, 256, 128
FLOPS = 2 * K * N * E * C

P = 128
PACK = 4
PASSES = K // (P * PACK)
SLOTS = E * C

F32 = mybir.dt.float32
BF16 = mybir.dt.bfloat16
I32 = mybir.dt.int32
U32 = mybir.dt.uint32
U16 = mybir.dt.uint16
U8 = mybir.dt.uint8
FP8X4 = mybir.dt.float8_e4m3fn_x4
MULT = mybir.AluOpType.mult
ADD = mybir.AluOpType.add

HALF = T // 2
VEC_TOKENS = 304
OUT_CUT = 320

GROUPS = ((0, 256), (256, 256), (512, 256), (768, 128), (896, 128))
CUTS = (384, 384, 256)
LAST_CUTS = (384, 384, 192, 64)


def tile_routed_moe_kernel(tc, xT, w_words, w_scales, gate, offs, pos1, pos2, out):
    nc = tc.nc
    with ExitStack() as ctx:
        held = ctx.enter_context(tc.tile_pool(name="held", bufs=1))
        psum = ctx.enter_context(tc.psum_pool(name="psum", bufs=1))

        offs_sb = held.tile([P, SLOTS // 16], U16, name="offs_sb")
        pos1_sb = held.tile([P, T // 16], U16, name="pos1_sb")
        pos2_sb = held.tile([P, T // 16], U16, name="pos2_sb")
        w_sb = held.tile([P, E, PASSES, N], U32, name="w_sb", align_bytes=64)
        ws_sb = held.tile([P, E, PASSES, N], U8, name="ws_sb", align_bytes=64)
        gate_sb = held.tile([P, 2, T], F32, name="gate_sb", align_bytes=64)
        xs = held.tile([P, T], U8, name="xs", align_bytes=64)
        gs = held.tile([P, SLOTS], U8, name="gs", align_bytes=64)
        y_sb = held.tile([P, SLOTS], F32, name="y_sb", align_bytes=64)
        raw0 = held.tile([P, PACK, T], F32, name="raw0", align_bytes=64)
        raw1 = [held.tile([P, PACK, HALF], F32, name=f"raw1{h}", align_bytes=64) for h in range(2)]
        grouped = [held.tile([P, T, PACK], BF16, name=f"grouped{a}", align_bytes=64) for a in range(PASSES)]
        xw = [held.tile([P, T], U32, name=f"xw{a}", align_bytes=64) for a in range(PASSES)]
        gw = [held.tile([P, SLOTS], U32, name=f"gw{a}", align_bytes=64) for a in range(PASSES)]

        warm = held.tile([P, 8], F32, name="warm")
        nc.vector.memset(warm[:], 0.0)
        nc.scalar.copy(warm[:, 4:8], warm[:, 0:4])
        nc.gpsimd.memset(xs[:], 0)
        nc.vector.memset(ws_sb[:].rearrange("p e a n -> p (e a n)").bitcast(I32), 0)

        nc.sync.dma_start(out=raw0[:], in_=xT[0:512, :].rearrange("(p t) n -> p t n", t=PACK))
        nc.sync.dma_start(offs_sb[:], offs)
        for h in range(2):
            rows = xT[512:1024, HALF * h : HALF * (h + 1)]
            nc.sync.dma_start(out=raw1[h][:], in_=rows.rearrange("(p t) n -> p t n", t=PACK))
        nc.sync.dma_start(
            out=w_sb[:].rearrange("p e a n -> p (e a) n").bitcast(I32),
            in_=w_words.rearrange("e a p n r -> p (e a) (n r)").bitcast(I32),
        )
        for q in range(4):
            nc.sync.dma_start(
                out=ws_sb[32 * q : 32 * q + 4].rearrange("p e a n -> p (e a) n").bitcast(I32),
                in_=w_scales[:, :, 4 * q : 4 * q + 4, :].rearrange("e a r n -> r (e a) n").bitcast(I32),
            )
        nc.sync.dma_start(pos1_sb[:], pos1)
        nc.sync.dma_start(pos2_sb[:], pos2)
        nc.sync.dma_start(out=gate_sb[:], in_=gate.rearrange("s p n -> p s n"))

        def interleave(copy, dst, src):
            copy(dst.rearrange("p (c i) t -> p c t i", i=4), src.rearrange("p t (c i) -> p c t i", i=4))

        def quantize(a, h):
            cols = slice(HALF * h, HALF * (h + 1))
            nc.vector.quantize_mx(
                out=xw[a][:, cols].bitcast(FP8X4),
                scales=xs[4 * a :, cols],
                in_=grouped[a][:, cols, :].rearrange("p n t -> p (n t)"),
            )

        def gather(dst, src, cuts):
            lo = 0
            for n in cuts:
                nc.vector.tensor_copy(dst[:, lo : lo + n], src[:].indirect(offs_sb[:, lo // 16 : (lo + n) // 16]))
                lo += n

        for lo, hi, copy in ((0, HALF, nc.vector.tensor_copy), (HALF, VEC_TOKENS, nc.vector.tensor_copy), (VEC_TOKENS, T, nc.scalar.copy)):
            interleave(copy, grouped[0][:, lo:hi, :], raw0[:, :, lo:hi])
        for h in range(2):
            quantize(0, h)
        for h in range(2):
            interleave(nc.scalar.copy, grouped[1][:, HALF * h : HALF * (h + 1), :], raw1[h][:])
        gather(gw[0], xw[0], CUTS)
        for h in range(2):
            quantize(1, h)
        gather(gs, xs, CUTS)
        gather(gw[1], xw[1], LAST_CUTS)

        banks = [psum.tile([P, n], F32, name=f"bank{i}") for i, (lo, n) in enumerate(GROUPS)]

        for a in range(PASSES):
            for i, (lo, n) in enumerate(GROUPS):
                nc.tensor.matmul_mx(
                    out=banks[i][:],
                    lhsT=w_sb[:, lo // C, a, :].bitcast(FP8X4),
                    lhsT_scale=ws_sb[:, lo // C, a, :],
                    rhs=gw[a][:, lo : lo + n].bitcast(FP8X4),
                    rhs_scale=gs[4 * a :, lo : lo + n],
                    start=(a == 0),
                    stop=(a == PASSES - 1),
                )
        for i, (lo, n) in enumerate(GROUPS):
            nc.scalar.copy(y_sb[:, lo : lo + n], banks[i][:])

        part1 = held.tile([P, T], F32, name="part1", align_bytes=64)
        part2 = held.tile([P, T], F32, name="part2", align_bytes=64)
        result = held.tile([P, T], F32, name="result", align_bytes=64)
        spans = ((0, OUT_CUT), (OUT_CUT, T))
        nc.vector.tensor_tensor(part1[:], y_sb[:].indirect(pos1_sb[:]), gate_sb[:, 0, :], MULT)
        for lo, hi in spans:
            nc.vector.tensor_tensor(
                part2[:, lo:hi], y_sb[:].indirect(pos2_sb[:, lo // 16 : hi // 16]), gate_sb[:, 1, lo:hi], MULT
            )
        for lo, hi in spans:
            nc.vector.tensor_tensor(result[:, lo:hi], part1[:, lo:hi], part2[:, lo:hi], ADD)
            nc.sync.dma_start(out=out[:, lo:hi], in_=result[:, lo:hi])
